import numpy as np, ml_dtypes
CORES = [13,21,141,149]
N = 4
import mx_ref
NC = 256
BF = ml_dtypes.bfloat16
def cut(t, i, w=512):
    return t[:, w * i:w * i + w]
def term(a, B):
    return np.stack([mx_ref.matmul(mx_ref.quantize(cut(a, i)), B) for i in range(4)], axis=2).reshape(128, -1)
def setup_inputs(rng):
    def f(*shape):
        return mx_ref.flush((rng.standard_normal(shape, dtype=np.float32) * np.exp2(rng.integers(-2, 3, shape[:-1] + (1,)))).astype(BF))
    return {"a": f(N, 128, 4 * 512), "b": f(N, 128, 2 * 4 * NC)}
def setup_inputs_blocks(rng):
    d = setup_inputs(rng)
    for k in ("a", "b"): d[k] = mx_ref.spread(d[k], rng, 2)
    return d
def setup_inputs_wide(rng):
    d = setup_inputs(rng)
    for k in ("a", "b"): d[k] = mx_ref.flush((d[k].astype(np.float32) * np.exp2(rng.integers(-4, 5, (N, 1, 1))).astype(np.float32)).astype(BF))
    return d
def setup_inputs_lossless(rng):
    a = np.zeros((N, 128, 4 * 128, 4), np.float32)
    for r in range(N):
        k = rng.integers(0, 512, size=4 * 128)
        a[r, k // 4, np.arange(4 * 128), k % 4] = 1.0
    size = np.tile(np.repeat(2.0 ** rng.integers(-4, 5, size=(1, 1, NC)), 4, axis=2), (1, 1, 2))
    b = rng.integers(-1, 2, size=(N, 128, 2 * 4 * NC)) * size
    return {"a": a.reshape(N, 128, 4 * 512).astype(BF), "b": b.astype(np.float32).astype(BF)}
def reference(a, b):
    T = [term(a[r], mx_ref.quantize(cut(b[r], k, 4 * NC))) for r in range(N) for k in range(2)]
    y = np.zeros((N, 128, 4 * NC), np.float32)
    for c in range(N):
        y[c] = mx_ref.total(T[:2 * c + 2])
    return {"y": y}

@@ -1,0 +1,204 @@
+from concourse.bass import DstId, RemoteDMATransfer
+from concourse.mybir import dt, AluOpType, ActivationFunctionType
+
+HC = 128
+X4 = "float8_e4m3fn_x4"
+SCRATCH = {
+    "at": ("sbuf", [128, 2048], "bfloat16"), "bt": ("sbuf", [128, 2048], "bfloat16"),
+    "aq": ("sbuf", [128, 512], X4), "ap": ("sbuf", [128, 512], "uint8"),
+    "bq": ("sbuf", [128, 512], X4), "bp": ("sbuf", [128, 512], "uint8"),
+    "one": ("sbuf", [128, 516], "bfloat16"), "eye": ("sbuf", [128, 516], "bfloat16"),
+    "wq": ("sbuf", [128, 512], X4), "wp": ("sbuf", [128, 512], "uint8"),
+    "st": ("sbuf", [128, 1024], "bfloat16"),
+    "sq": ("sbuf", [128, 256], X4), "sp": ("sbuf", [128, 256], "uint8"),
+    "dq": ("sbuf", [128, 256], X4), "dp": ("sbuf", [128, 256], "uint8"),
+    "rq": ("sbuf", [128, 256], X4), "rp": ("sbuf", [128, 256], "uint8"),
+    "yt": ("sbuf", [128, 1024], "float32"),
+    "ps": ("psum", [128, 4096], "float32"),
+}
+SEMAPHORES = (["one", "eye", "la0", "la1", "sent", "stored", "d"]
+              + ["lb%d%d" % (k, h) for k in range(2) for h in range(2)]
+              + ["w%d" % t for t in range(4)] + ["a%d" % i for i in range(4)]
+              + ["b%d%d" % (k, h) for k in range(2) for h in range(2)]
+              + ["%s%d%d" % (s, h, i) for s in ("m", "c", "u", "e") for h in range(2) for i in range(4)]
+              + ["%s%d" % (s, h) for s in ("q", "d", "rc", "rs") for h in range(2)])
+
+
+def _relay(src, dst, T, topo):
+    for c in range(256):
+        if (c not in T.cores and topo.host(c) == topo.host(src) and topo.chip(c) == topo.chip(src)
+                and topo.die(c) == topo.die(src) and topo.may_write(c, dst)):
+            return c
+
+
+def rank_program(g, core, T, topo):
+    C = list(T.cores)
+    rank = T.rank_of(core)
+    r0, r1, add = _relay(C[0], C[1], T, topo), _relay(C[1], C[2], T, topo), _relay(C[2], C[3], T, topo)
+    sem = T.sem
+    sent = [0]
+
+    def half(t, h):
+        return t[:, HC * h:HC * h + HC]
+
+    def codes(ap):
+        return ap.bitcast(dt.uint8)
+
+    def move(pairs):
+        trs = []
+        for dst, mask, s, a, b in pairs:
+            rid, pnc = topo.addr(dst, core)
+            trs.append(RemoteDMATransfer(dst_ids=[DstId(rid=rid, pnc=pnc)], dma_engine_mask=mask,
+                                         remote_sem=sem[s], src=a, dst=b))
+            sent[0] += bin(mask).count("1")
+        g.remote_dma_fused(trs, local_sem=sem.sent)
+
+    def bits(mask):
+        return bin(mask).count("1")
+
+    off_mask = topo.mask(C[0], C[2])
+    on_mask = topo.mask(C[0], r0) & ~off_mask
+    ND, NR = bits(off_mask), bits(on_mask)
+
+    if core in (r0, r1):
+        dst = C[1] if core == r0 else C[2]
+        m = topo.mask(core, dst)
+        for h in range(2):
+            g.wait_ge(sem["rc%d" % h], NR)
+            move([(dst, m, "rc%d" % h, codes(half(T.rq, h)), codes(half(T.rq, h)))])
+            g.wait_ge(sem["rs%d" % h], NR)
+            move([(dst, m, "rs%d" % h, half(T.rp, h), half(T.rp, h))])
+        g.wait_ge(sem.sent, sent[0])
+        return
+    if rank is None and core != add:
+        return
+
+    V, S, P = g.vector, g.scalar, g.tensor
+    COPY = ActivationFunctionType.Copy
+
+    if rank is not None:
+        g.sync.dma_start(T.at[:, 0:1024], T.a[:, 0:1024]).then_inc(sem.la0, 16)
+        S.dma_start(T.at[:, 1024:2048], T.a[:, 1024:2048]).then_inc(sem.la1, 16)
+        for h in range(2):
+            for k, q in ((0, g.sync), (1, S)):
+                o = 1024 * k + 512 * h
+                q.dma_start(T.bt[:, o:o + 512], T.b[:, o:o + 512]).then_inc(sem["lb%d%d" % (k, h)], 16)
+
+    if rank != 0:
+        V.memset(T.one[:], 1.0).then_inc(sem.one, 1)
+        g.wait_ge(sem.one, 1)
+        g.affine_select(T.eye[:], T.one[:], [[-1, 516]], AluOpType.is_equal, 0.0, 3, 4).then_inc(sem.eye, 1)
+        V.wait_ge(sem.eye, 1)
+        for t in range(4):
+            V.quantize_mx(T.wq[:, 128 * t:128 * t + 128], T.wp[:, 128 * t:128 * t + 128],
+                          T.eye[:, 3 - t:515 - t]).then_inc(sem["w%d" % t], 1)
+
+    def bank(h, i):
+        o = 512 * (4 * h + i)
+        return T.ps[:, o:o + HC]
+
+    def unpack(q, p, h, start, stop, done=None, first=False):
+        for t in range(4):
+            if first:
+                P.wait_ge(sem["w%d" % t], 1)
+            x = P.matmul_mx(bank(h, t), T.wq[:, 128 * t:128 * t + 128], T.wp[:, 128 * t:128 * t + 128],
+                            half(q, h), half(p, h), start, stop)
+            if done:
+                x.then_inc(sem["%s%d%d" % (done, h, t)], 1)
+
+    def product(h, k, i, stop):
+        o = 256 * k + HC * h
+        return P.matmul_mx(bank(h, i), T.aq[:, 128 * i:128 * i + 128], T.ap[:, 128 * i:128 * i + 128],
+                           T.bq[:, o:o + HC], T.bp[:, o:o + HC], k == 0, stop)
+
+    def cast_and_pack(h):
+        for i in range(4):
+            out = T.st[:, 512 * h + i:512 * h + 512:4]
+            (V if i % 2 == 0 else S).wait_ge(sem["m%d%d" % (h, i)], 1)
+            if i % 2 == 0:
+                V.tensor_copy(out, bank(h, i)).then_inc(sem["c%d%d" % (h, i)], 1)
+            else:
+                S.activation(out, bank(h, i), COPY).then_inc(sem["c%d%d" % (h, i)], 1)
+        for i in range(4):
+            V.wait_ge(sem["c%d%d" % (h, i)], 1)
+        V.quantize_mx(half(T.sq, h), half(T.sp, h), T.st[:, 512 * h:512 * h + 512]).then_inc(sem["q%d" % h], 1)
+
+    if core == add:
+        for h in range(2):
+            P.wait_ge(sem["rc%d" % h], NR)
+            P.wait_ge(sem["rs%d" % h], NR)
+            unpack(T.rq, T.rp, h, True, False, first=(h == 0))
+            P.wait_ge(sem["d%d" % h], 2 * ND)
+            unpack(T.dq, T.dp, h, False, True, done="m")
+            cast_and_pack(h)
+            m = topo.mask(core, C[3])
+            g.wait_ge(sem["q%d" % h], 1)
+            move([(C[3], m, "rc%d" % h, codes(half(T.sq, h)), codes(half(T.rq, h)))])
+            move([(C[3], m, "rs%d" % h, half(T.sp, h), half(T.rp, h))])
+        g.wait_ge(sem.sent, sent[0])
+        return
+
+    for i in range(4):
+        if i % 2 == 0:
+            V.wait_ge(sem["la%d" % (i // 2)], 16)
+        V.quantize_mx(T.aq[:, 128 * i:128 * i + 128], T.ap[:, 128 * i:128 * i + 128],
+                      T.at[:, 512 * i:512 * i + 512]).then_inc(sem["a%d" % i], 1)
+    for h in range(2):
+        for k in range(2):
+            o = 256 * k + HC * h
+            V.wait_ge(sem["lb%d%d" % (k, h)], 16)
+            V.quantize_mx(T.bq[:, o:o + HC], T.bp[:, o:o + HC],
+                          T.bt[:, 4 * o:4 * o + 512]).then_inc(sem["b%d%d" % (k, h)], 1)
+            P.wait_ge(sem["b%d%d" % (k, h)], 1)
+            for i in range(4):
+                if h == 0 and k == 0:
+                    P.wait_ge(sem["a%d" % i], 1)
+                x = product(h, k, i, k == 1 and rank != 3)
+                if k == 1 and rank != 3:
+                    x.then_inc(sem["m%d%d" % (h, i)], 1)
+        if rank == 3:
+            continue
+        cast_and_pack(h)
+        g.wait_ge(sem["q%d" % h], 1)
+        if rank == 0:
+            move([(add, off_mask, "d%d" % h, codes(half(T.sq, h)), codes(half(T.dq, h))),
+                  (r0, on_mask, "rc%d" % h, codes(half(T.sq, h)), codes(half(T.rq, h)))])
+            move([(add, off_mask, "d%d" % h, half(T.sp, h), half(T.dp, h)),
+                  (r0, on_mask, "rs%d" % h, half(T.sp, h), half(T.rp, h))])
+        else:
+            d = r1 if rank == 1 else add
+            move([(d, on_mask, "rc%d" % h, codes(half(T.sq, h)), codes(half(T.rq, h)))])
+            move([(d, on_mask, "rs%d" % h, half(T.sp, h), half(T.rp, h))])
+    if rank < 2:
+        move([(C[rank + 2], off_mask, "d", codes(T.sq[:, 0:256]), codes(T.dq[:, 0:256]))])
+        move([(C[rank + 2], off_mask, "d", T.sp[:, 0:256], T.dp[:, 0:256])])
+
+    if rank in (1, 2):
+        for h in range(2):
+            for i in range(4):
+                P.wait_ge(sem["c%d%d" % (h, i)], 1)
+                for k in range(2):
+                    product(h, k, i, False)
+    for h in range(2):
+        if rank > 0:
+            if rank >= 2:
+                if h == 0:
+                    P.wait_ge(sem.d, 2 * ND)
+                unpack(T.dq, T.dp, h, False, False, first=(h == 0))
+            P.wait_ge(sem["rc%d" % h], ND)
+            P.wait_ge(sem["rs%d" % h], ND)
+            unpack(T.rq, T.rp, h, False, True, done="u", first=(rank == 1 and h == 0))
+        for i in range(4):
+            out = T.yt[:, 512 * h + i:512 * h + 512:4]
+            e = V if i % 2 == 0 else S
+            e.wait_ge(sem["%s%d%d" % ("u" if rank else "m", h, i)], 1)
+            if i % 2 == 0:
+                V.tensor_copy(out, bank(h, i)).then_inc(sem["e%d%d" % (h, i)], 1)
+            else:
+                S.activation(out, bank(h, i), COPY).then_inc(sem["e%d%d" % (h, i)], 1)
+        for i in range(4):
+            g.sync.wait_ge(sem["e%d%d" % (h, i)], 1)
+        g.sync.dma_start(T.y[:, 512 * h:512 * h + 512], T.yt[:, 512 * h:512 * h + 512]).then_inc(sem.stored, 16)
+    if sent[0]:
+        g.wait_ge(sem.sent, sent[0])
+    g.sync.wait_ge(sem.stored, 32)

@@ -13,21 +13,22 @@ SCRATCH = {
     "sq": ("sbuf", [128, 256], X4), "sp": ("sbuf", [128, 256], "uint8"),
     "dq": ("sbuf", [128, 256], X4), "dp": ("sbuf", [128, 256], "uint8"),
     "rq": ("sbuf", [128, 256], X4), "rp": ("sbuf", [128, 256], "uint8"),
+    "xq": ("sbuf", [128, 128], X4), "xp": ("sbuf", [128, 128], "uint8"),
     "yt": ("sbuf", [128, 1024], "float32"),
     "ps": ("psum", [128, 4096], "float32"),
 }
-SEMAPHORES = (["one", "eye", "la0", "la1", "sent", "stored", "d"]
+SEMAPHORES = (["one", "eye", "la0", "la1", "sent", "stored", "d", "xc", "xs"]
               + ["lb%d%d" % (k, h) for k in range(2) for h in range(2)]
-              + ["w%d" % t for t in range(4)] + ["a%d" % i for i in range(4)]
+              + ["w%d" % t for t in range(4)] + ["wr%d" % t for t in range(4)] + ["a%d" % i for i in range(4)]
               + ["b%d%d" % (k, h) for k in range(2) for h in range(2)]
               + ["%s%d%d" % (s, h, i) for s in ("m", "c", "u", "e") for h in range(2) for i in range(4)]
               + ["%s%d" % (s, h) for s in ("q", "d", "rc", "rs") for h in range(2)])
 
 
-def _relay(src, dst, T, topo):
+def _relay(src, dst, T, topo, same=True):
     for c in range(256):
         if (c not in T.cores and topo.host(c) == topo.host(src) and topo.chip(c) == topo.chip(src)
-                and topo.die(c) == topo.die(src) and topo.may_write(c, dst)):
+                and (topo.die(c) == topo.die(src)) == same and topo.may_write(c, dst)):
             return c
 
 
@@ -35,8 +36,13 @@ def rank_program(g, core, T, topo):
     C = list(T.cores)
     rank = T.rank_of(core)
     r0, r1, add = _relay(C[0], C[1], T, topo), _relay(C[1], C[2], T, topo), _relay(C[2], C[3], T, topo)
+    r0b, r2 = _relay(C[0], C[3], T, topo, False), _relay(C[2], C[3], T, topo, False)
+    lend = {r0: (C[1], 0), r1: (C[1], 1), add: (C[2], 3), r0b: (add, 0), r2: (add, 1), C[0]: (add, 2)}
     sem = T.sem
     sent = [0]
+
+    def bits(mask):
+        return bin(mask).count("1")
 
     def half(t, h):
         return t[:, HC * h:HC * h + HC]
@@ -44,30 +50,51 @@ def rank_program(g, core, T, topo):
     def codes(ap):
         return ap.bitcast(dt.uint8)
 
-    def move(pairs):
+    def move(*pairs):
         trs = []
-        for dst, mask, s, a, b in pairs:
-            rid, pnc = topo.addr(dst, core)
-            trs.append(RemoteDMATransfer(dst_ids=[DstId(rid=rid, pnc=pnc)], dma_engine_mask=mask,
-                                         remote_sem=sem[s], src=a, dst=b))
-            sent[0] += bin(mask).count("1")
+        for d, mask, s, a, b in pairs:
+            rid, pnc = topo.addr(d, core)
+            trs.append(RemoteDMATransfer(dst_ids=[DstId(rid=rid, pnc=pnc)], dma_engine_mask=mask, remote_sem=sem[s],
+                                         src=a, dst=b))
+            sent[0] += bits(mask)
         g.remote_dma_fused(trs, local_sem=sem.sent)
-
-    def bits(mask):
-        return bin(mask).count("1")
 
     off_mask = topo.mask(C[0], C[2])
     on_mask = topo.mask(C[0], r0) & ~off_mask
     ND, NR = bits(off_mask), bits(on_mask)
 
-    if core in (r0, r1):
-        dst = C[1] if core == r0 else C[2]
-        m = topo.mask(core, dst)
-        for h in range(2):
+    lent = [t for d, t in lend.values() if d == core]
+
+    def wpart(t):
+        return T.wq[:, 128 * t:128 * t + 128], T.wp[:, 128 * t:128 * t + 128]
+
+    def constants(ts):
+        g.vector.memset(T.one[:], 1.0).then_inc(sem.one, 1)
+        g.wait_ge(sem.one, 1)
+        g.affine_select(T.eye[:], T.one[:], [[-1, 516]], AluOpType.is_equal, 0.0, 3, 4).then_inc(sem.eye, 1)
+        g.vector.wait_ge(sem.eye, 1)
+        for t in ts:
+            q, p = wpart(t)
+            g.vector.quantize_mx(q, p, T.eye[:, 3 - t:515 - t]).then_inc(sem["w%d" % t], 1)
+        if core in lend:
+            d, t = lend[core]
+            q, p = wpart(t)
+            g.wait_ge(sem["w%d" % t], 1)
+            move((d, off_mask, "wr%d" % t, codes(q), codes(q)))
+            move((d, off_mask, "wr%d" % t, p, p))
+
+    if core in (r0, r1, r0b, r2):
+        dst = {r0: C[1], r1: C[2], r0b: C[3], r2: C[3]}[core]
+        constants([lend[core][1]])
+        for h in (0, 1) if core in (r0, r1) else (1,):
+            q, p, s = (half(T.rq, h), half(T.rp, h), "r%s" + str(h)) if core != r2 else (half(T.xq, 0), half(T.xp, 0), "x%s")
             g.wait_ge(sem["rc%d" % h], NR)
-            move([(dst, m, "rc%d" % h, codes(half(T.rq, h)), codes(half(T.rq, h)))])
+            move((dst, off_mask, s % "c", codes(half(T.rq, h)), codes(q)))
             g.wait_ge(sem["rs%d" % h], NR)
-            move([(dst, m, "rs%d" % h, half(T.rp, h), half(T.rp, h))])
+            move((dst, off_mask, s % "s", half(T.rp, h), p))
+        if core == r0b:
+            move((C[2], off_mask, "d1", codes(half(T.rq, 1)), codes(half(T.dq, 1))))
+            move((C[2], off_mask, "d1", half(T.rp, 1), half(T.dp, 1)))
         g.wait_ge(sem.sent, sent[0])
         return
     if rank is None and core != add:
@@ -76,33 +103,22 @@ def rank_program(g, core, T, topo):
     V, S, P = g.vector, g.scalar, g.tensor
     COPY = ActivationFunctionType.Copy
 
-    if rank is not None:
-        g.sync.dma_start(T.at[:, 0:1024], T.a[:, 0:1024]).then_inc(sem.la0, 16)
-        S.dma_start(T.at[:, 1024:2048], T.a[:, 1024:2048]).then_inc(sem.la1, 16)
-        for h in range(2):
-            for k, q in ((0, g.sync), (1, S)):
-                o = 1024 * k + 512 * h
-                q.dma_start(T.bt[:, o:o + 512], T.b[:, o:o + 512]).then_inc(sem["lb%d%d" % (k, h)], 16)
-
-    if rank != 0:
-        V.memset(T.one[:], 1.0).then_inc(sem.one, 1)
-        g.wait_ge(sem.one, 1)
-        g.affine_select(T.eye[:], T.one[:], [[-1, 516]], AluOpType.is_equal, 0.0, 3, 4).then_inc(sem.eye, 1)
-        V.wait_ge(sem.eye, 1)
-        for t in range(4):
-            V.quantize_mx(T.wq[:, 128 * t:128 * t + 128], T.wp[:, 128 * t:128 * t + 128],
-                          T.eye[:, 3 - t:515 - t]).then_inc(sem["w%d" % t], 1)
-
     def bank(h, i):
         o = 512 * (4 * h + i)
         return T.ps[:, o:o + HC]
 
-    def unpack(q, p, h, start, stop, done=None, first=False):
+    known = {}
+
+    def unpack(q, p, h, start, stop, done=None):
         for t in range(4):
-            if first:
-                P.wait_ge(sem["w%d" % t], 1)
-            x = P.matmul_mx(bank(h, t), T.wq[:, 128 * t:128 * t + 128], T.wp[:, 128 * t:128 * t + 128],
-                            half(q, h), half(p, h), start, stop)
+            if t not in known:
+                known[t] = 1
+                if t in lent:
+                    P.wait_ge(sem["wr%d" % t], 2 * ND)
+                else:
+                    P.wait_ge(sem["w%d" % t], 1)
+            wq, wp = wpart(t)
+            x = P.matmul_mx(bank(h, t), wq, wp, q, p, start, stop)
             if done:
                 x.then_inc(sem["%s%d%d" % (done, h, t)], 1)
 
@@ -123,55 +139,105 @@ def rank_program(g, core, T, topo):
             V.wait_ge(sem["c%d%d" % (h, i)], 1)
         V.quantize_mx(half(T.sq, h), half(T.sp, h), T.st[:, 512 * h:512 * h + 512]).then_inc(sem["q%d" % h], 1)
 
+    def load_a(j):
+        g.sync.dma_start(T.at[:, 1024 * j:1024 * j + 1024], T.a[:, 1024 * j:1024 * j + 1024]).then_inc(sem["la%d" % j], 16)
+
+    def load_b(k, h):
+        o = 1024 * k + 512 * h
+        g.sync.dma_start(T.bt[:, o:o + 512], T.b[:, o:o + 512]).then_inc(sem["lb%d%d" % (k, h)], 16)
+
+    if rank is not None:
+        load_a(0)
+        load_b(0, 0)
+        load_b(1, 0)
+        load_a(1)
+        load_b(0, 1)
+        load_b(1, 1)
+
+    if rank == 0:
+        constants([lend[core][1]])
+    else:
+        constants([t for t in (3, 0, 1, 2) if t not in lent])
+
     if core == add:
-        for h in range(2):
-            P.wait_ge(sem["rc%d" % h], NR)
-            P.wait_ge(sem["rs%d" % h], NR)
-            unpack(T.rq, T.rp, h, True, False, first=(h == 0))
-            P.wait_ge(sem["d%d" % h], 2 * ND)
-            unpack(T.dq, T.dp, h, False, True, done="m")
-            cast_and_pack(h)
-            m = topo.mask(core, C[3])
-            g.wait_ge(sem["q%d" % h], 1)
-            move([(C[3], m, "rc%d" % h, codes(half(T.sq, h)), codes(half(T.rq, h)))])
-            move([(C[3], m, "rs%d" % h, half(T.sp, h), half(T.rp, h))])
+        P.wait_ge(sem.rc0, NR)
+        P.wait_ge(sem.rs0, NR)
+        unpack(half(T.rq, 0), half(T.rp, 0), 0, True, False)
+        P.wait_ge(sem.d0, 2 * ND)
+        unpack(half(T.dq, 0), half(T.dp, 0), 0, False, True, done="m")
+        cast_and_pack(0)
+        g.wait_ge(sem.q0, 1)
+        move((C[3], off_mask, "rc0", codes(half(T.sq, 0)), codes(half(T.rq, 0))))
+        move((C[3], off_mask, "rs0", half(T.sp, 0), half(T.rp, 0)))
         g.wait_ge(sem.sent, sent[0])
         return
 
-    for i in range(4):
+    def pack_a(i):
         if i % 2 == 0:
             V.wait_ge(sem["la%d" % (i // 2)], 16)
         V.quantize_mx(T.aq[:, 128 * i:128 * i + 128], T.ap[:, 128 * i:128 * i + 128],
                       T.at[:, 512 * i:512 * i + 512]).then_inc(sem["a%d" % i], 1)
-    for h in range(2):
-        for k in range(2):
-            o = 256 * k + HC * h
-            V.wait_ge(sem["lb%d%d" % (k, h)], 16)
-            V.quantize_mx(T.bq[:, o:o + HC], T.bp[:, o:o + HC],
-                          T.bt[:, 4 * o:4 * o + 512]).then_inc(sem["b%d%d" % (k, h)], 1)
-            P.wait_ge(sem["b%d%d" % (k, h)], 1)
-            for i in range(4):
-                if h == 0 and k == 0:
-                    P.wait_ge(sem["a%d" % i], 1)
-                x = product(h, k, i, k == 1 and rank != 3)
-                if k == 1 and rank != 3:
-                    x.then_inc(sem["m%d%d" % (h, i)], 1)
-        if rank == 3:
-            continue
-        cast_and_pack(h)
+
+    def pack_b(k, h):
+        o = 256 * k + HC * h
+        V.wait_ge(sem["lb%d%d" % (k, h)], 16)
+        V.quantize_mx(T.bq[:, o:o + HC], T.bp[:, o:o + HC],
+                      T.bt[:, 4 * o:4 * o + 512]).then_inc(sem["b%d%d" % (k, h)], 1)
+
+    def own(h, k, i):
+        x = product(h, k, i, k == 1 and rank != 3)
+        if k == 1 and rank != 3:
+            x.then_inc(sem["m%d%d" % (h, i)], 1)
+
+    def send(h):
         g.wait_ge(sem["q%d" % h], 1)
-        if rank == 0:
-            move([(add, off_mask, "d%d" % h, codes(half(T.sq, h)), codes(half(T.dq, h))),
-                  (r0, on_mask, "rc%d" % h, codes(half(T.sq, h)), codes(half(T.rq, h)))])
-            move([(add, off_mask, "d%d" % h, half(T.sp, h), half(T.dp, h)),
-                  (r0, on_mask, "rs%d" % h, half(T.sp, h), half(T.rp, h))])
-        else:
-            d = r1 if rank == 1 else add
-            move([(d, on_mask, "rc%d" % h, codes(half(T.sq, h)), codes(half(T.rq, h)))])
-            move([(d, on_mask, "rs%d" % h, half(T.sp, h), half(T.rp, h))])
-    if rank < 2:
-        move([(C[rank + 2], off_mask, "d", codes(T.sq[:, 0:256]), codes(T.dq[:, 0:256]))])
-        move([(C[rank + 2], off_mask, "d", T.sp[:, 0:256], T.dp[:, 0:256])])
+        q, p = half(T.sq, h), half(T.sp, h)
+        near = {0: r0, 1: r1, 2: add if h == 0 else r2}[rank]
+        c = [(near, on_mask, "rc%d" % h, codes(q), codes(half(T.rq, h)))]
+        s = [(near, on_mask, "rs%d" % h, p, half(T.rp, h))]
+        if rank == 0 and h == 0:
+            c.append((add, off_mask, "d0", codes(q), codes(half(T.dq, 0))))
+            s.append((add, off_mask, "d0", p, half(T.dp, 0)))
+        if rank == 0 and h == 1:
+            c.append((r0b, off_mask, "rc1", codes(q), codes(half(T.rq, 1))))
+            s.append((r0b, off_mask, "rs1", p, half(T.rp, 1)))
+        move(*c)
+        move(*s)
+
+    pack_a(0)
+    pack_a(1)
+    pack_b(0, 0)
+    pack_b(1, 0)
+    pack_a(2)
+    pack_a(3)
+    for k in range(2):
+        P.wait_ge(sem["b%d0" % k], 1)
+        for i in (0, 1):
+            if k == 0:
+                P.wait_ge(sem["a%d" % i], 1)
+            own(0, k, i)
+    for i in (2, 3):
+        P.wait_ge(sem["a%d" % i], 1)
+        own(0, 0, i)
+        own(0, 1, i)
+    pack_b(0, 1)
+    if rank != 3:
+        cast_and_pack(0)
+        send(0)
+    pack_b(1, 1)
+    for k in range(2):
+        P.wait_ge(sem["b%d1" % k], 1)
+        for i in range(4):
+            own(1, k, i)
+    if rank != 3:
+        cast_and_pack(1)
+        send(1)
+    if rank == 0:
+        move((C[2], off_mask, "d0", codes(half(T.sq, 0)), codes(half(T.dq, 0))))
+        move((C[2], off_mask, "d0", half(T.sp, 0), half(T.dp, 0)))
+    elif rank == 1:
+        move((C[3], off_mask, "d", codes(T.sq[:, 0:256]), codes(T.dq[:, 0:256])))
+        move((C[3], off_mask, "d", T.sp[:, 0:256], T.dp[:, 0:256]))
 
     if rank in (1, 2):
         for h in range(2):
@@ -179,15 +245,16 @@ def rank_program(g, core, T, topo):
                 P.wait_ge(sem["c%d%d" % (h, i)], 1)
                 for k in range(2):
                     product(h, k, i, False)
-    for h in range(2):
-        if rank > 0:
-            if rank >= 2:
-                if h == 0:
-                    P.wait_ge(sem.d, 2 * ND)
-                unpack(T.dq, T.dp, h, False, False, first=(h == 0))
-            P.wait_ge(sem["rc%d" % h], ND)
-            P.wait_ge(sem["rs%d" % h], ND)
-            unpack(T.rq, T.rp, h, False, True, done="u", first=(rank == 1 and h == 0))
+
+    def relayed(h, stop):
+        P.wait_ge(sem["rc%d" % h], ND)
+        P.wait_ge(sem["rs%d" % h], ND)
+        unpack(half(T.rq, h), half(T.rp, h), h, False, stop, done="u" if stop else None)
+
+    def direct(h, stop):
+        unpack(half(T.dq, h), half(T.dp, h), h, False, stop, done="u" if stop else None)
+
+    def finish(h):
         for i in range(4):
             out = T.yt[:, 512 * h + i:512 * h + 512:4]
             e = V if i % 2 == 0 else S
@@ -199,6 +266,30 @@ def rank_program(g, core, T, topo):
         for i in range(4):
             g.sync.wait_ge(sem["e%d%d" % (h, i)], 1)
         g.sync.dma_start(T.y[:, 512 * h:512 * h + 512], T.yt[:, 512 * h:512 * h + 512]).then_inc(sem.stored, 16)
+
+    if rank == 0:
+        finish(0)
+        finish(1)
+    elif rank == 1:
+        for h in range(2):
+            relayed(h, True)
+            finish(h)
+    elif rank == 2:
+        for h in range(2):
+            relayed(h, False)
+            P.wait_ge(sem["d%d" % h], 2 * ND)
+            direct(h, True)
+            finish(h)
+    else:
+        P.wait_ge(sem.d, 2 * ND)
+        direct(0, False)
+        direct(1, False)
+        P.wait_ge(sem.xc, ND)
+        P.wait_ge(sem.xs, ND)
+        unpack(T.xq[:, 0:HC], T.xp[:, 0:HC], 1, False, False)
+        for h in (1, 0):
+            relayed(h, True)
+            finish(h)
     if sent[0]:
         g.wait_ge(sem.sent, sent[0])
     g.sync.wait_ge(sem.stored, 32)

@@ -2,12 +2,13 @@ from concourse.bass import DstId, RemoteDMATransfer
 from concourse.mybir import dt, AluOpType, ActivationFunctionType
 
 HC = 128
+LW = 32
 X4 = "float8_e4m3fn_x4"
 SCRATCH = {
     "at": ("sbuf", [128, 2048], "bfloat16"), "bt": ("sbuf", [128, 2048], "bfloat16"),
     "aq": ("sbuf", [128, 512], X4), "ap": ("sbuf", [128, 512], "uint8"),
     "bq": ("sbuf", [128, 512], X4), "bp": ("sbuf", [128, 512], "uint8"),
-    "one": ("sbuf", [128, 516], "bfloat16"), "eye": ("sbuf", [128, 516], "bfloat16"),
+    "one": ("sbuf", [128, 128], "bfloat16"), "eye": ("sbuf", [128, 516], "bfloat16"),
     "wq": ("sbuf", [128, 512], X4), "wp": ("sbuf", [128, 512], "uint8"),
     "st": ("sbuf", [128, 1024], "bfloat16"),
     "sq": ("sbuf", [128, 256], X4), "sp": ("sbuf", [128, 256], "uint8"),
@@ -17,7 +18,7 @@ SCRATCH = {
     "yt": ("sbuf", [128, 1024], "float32"),
     "ps": ("psum", [128, 4096], "float32"),
 }
-SEMAPHORES = (["one", "eye", "la0", "la1", "sent", "stored", "d", "xc", "xs"]
+SEMAPHORES = (["one", "eye", "la0", "la2", "la3", "sent", "stored", "xc", "xs", "wf0", "wf1"]
               + ["lb%d%d" % (k, h) for k in range(2) for h in range(2)]
               + ["w%d" % t for t in range(4)] + ["wr%d" % t for t in range(4)] + ["a%d" % i for i in range(4)]
               + ["b%d%d" % (k, h) for k in range(2) for h in range(2)]
@@ -37,12 +38,29 @@ def rank_program(g, core, T, topo):
     rank = T.rank_of(core)
     r0, r1, add = _relay(C[0], C[1], T, topo), _relay(C[1], C[2], T, topo), _relay(C[2], C[3], T, topo)
     r0b, r2 = _relay(C[0], C[3], T, topo, False), _relay(C[2], C[3], T, topo, False)
-    lend = {r0: (C[1], 0), r1: (C[1], 1), add: (C[2], 3), r0b: (add, 0), r2: (add, 1), C[0]: (add, 2)}
     sem = T.sem
     sent = [0]
 
     def bits(mask):
         return bin(mask).count("1")
+
+    OFF = topo.mask(C[0], C[2])
+    ALL = topo.mask(C[0], r0)
+    ON = ALL & ~OFF
+    ND, NR = bits(OFF), bits(ON)
+    M, L = LW // 2, (LW + 128) // 2
+    lend = [(C[0], r0, C[1], 1, 0, LW, ON), (r0b, None, C[1], 1, LW, 128, OFF), (r0, None, C[1], 0, 0, 128, OFF),
+            (r1, None, C[1], 2, 0, 128, OFF),
+            (C[1], r1, C[2], 3, 0, M, ON), (C[1], r1, C[2], 3, M, LW, OFF),
+            (add, None, C[2], 3, LW, L, ON), (add, None, C[2], 3, L, 128, OFF),
+            (C[0], None, add, 1, 0, LW, OFF), (r2, None, add, 1, LW, 128, OFF),
+            (C[2], None, add, 2, 0, M, ON), (C[2], None, add, 2, M, LW, OFF), (r2, None, add, 2, LW, 128, OFF)]
+    mine = [x for x in lend if x[0] == core]
+    passed = [x for x in lend if x[1] == core]
+    makes = sorted({x[3] for x in mine})
+    lent = {}
+    for t, piece, n in {(x[3], x[1] or x[4], bits(OFF if x[1] else x[6])) for x in lend if x[2] == core}:
+        lent[t] = lent.get(t, 0) + 2 * n
 
     def half(t, h):
         return t[:, HC * h:HC * h + HC]
@@ -59,42 +77,44 @@ def rank_program(g, core, T, topo):
             sent[0] += bits(mask)
         g.remote_dma_fused(trs, local_sem=sem.sent)
 
-    off_mask = topo.mask(C[0], C[2])
-    on_mask = topo.mask(C[0], r0) & ~off_mask
-    ND, NR = bits(off_mask), bits(on_mask)
-
-    lent = [t for d, t in lend.values() if d == core]
-
     def wpart(t):
         return T.wq[:, 128 * t:128 * t + 128], T.wp[:, 128 * t:128 * t + 128]
 
+    def piece(t, lo, hi, n):
+        q, p = wpart(t)
+        return p[:, lo:hi] if n else codes(q[:, lo:hi])
+
     def constants(ts):
         g.vector.memset(T.one[:], 1.0).then_inc(sem.one, 1)
-        g.wait_ge(sem.one, 1)
-        g.affine_select(T.eye[:], T.one[:], [[-1, 516]], AluOpType.is_equal, 0.0, 3, 4).then_inc(sem.eye, 1)
+        g.vector.memset(T.eye[:], 0.0).then_inc(sem.one, 1)
+        g.wait_ge(sem.one, 2)
+        g.affine_select(T.eye[:, 3:515:4], T.one[:], [[-1, 128]], AluOpType.is_equal, 0.0, 0, 1).then_inc(sem.eye, 1)
         g.vector.wait_ge(sem.eye, 1)
         for t in ts:
             q, p = wpart(t)
             g.vector.quantize_mx(q, p, T.eye[:, 3 - t:515 - t]).then_inc(sem["w%d" % t], 1)
-        if core in lend:
-            d, t = lend[core]
-            q, p = wpart(t)
+        for t in makes:
             g.wait_ge(sem["w%d" % t], 1)
-            move((d, off_mask, "wr%d" % t, codes(q), codes(q)))
-            move((d, off_mask, "wr%d" % t, p, p))
+            for n in range(2):
+                move(*[(v or d, mask, "wf%d" % n if v else "wr%d" % t, piece(t, lo, hi, n), piece(t, lo, hi, n))
+                       for _, v, d, u, lo, hi, mask in mine if u == t])
+        if passed:
+            lo, hi, t, d = min(x[4] for x in passed), max(x[5] for x in passed), passed[0][3], passed[0][2]
+            for n in range(2):
+                g.wait_ge(sem["wf%d" % n], sum(bits(x[6]) for x in passed))
+                move((d, OFF, "wr%d" % t, piece(t, lo, hi, n), piece(t, lo, hi, n)))
 
+    relays = [(r0, 0, C[1]), (r0, 1, C[1]), (r0b, 1, C[3]), (r1, 0, C[2]), (r1, 1, C[2]), (r2, 1, C[3])]
     if core in (r0, r1, r0b, r2):
-        dst = {r0: C[1], r1: C[2], r0b: C[3], r2: C[3]}[core]
-        constants([lend[core][1]])
-        for h in (0, 1) if core in (r0, r1) else (1,):
-            q, p, s = (half(T.rq, h), half(T.rp, h), "r%s" + str(h)) if core != r2 else (half(T.xq, 0), half(T.xp, 0), "x%s")
-            g.wait_ge(sem["rc%d" % h], NR)
-            move((dst, off_mask, s % "c", codes(half(T.rq, h)), codes(q)))
-            g.wait_ge(sem["rs%d" % h], NR)
-            move((dst, off_mask, s % "s", half(T.rp, h), p))
-        if core == r0b:
-            move((C[2], off_mask, "d1", codes(half(T.rq, 1)), codes(half(T.dq, 1))))
-            move((C[2], off_mask, "d1", half(T.rp, 1), half(T.dp, 1)))
+        constants(makes)
+        n = ND + NR if core == r2 else NR
+        for c, h, dst in relays:
+            if c == core:
+                q, p, s = (half(T.rq, h), half(T.rp, h), "r%s" + str(h)) if core != r2 else (half(T.xq, 0), half(T.xp, 0), "x%s")
+                g.wait_ge(sem["rc%d" % h], n)
+                move((dst, OFF, s % "c", codes(half(T.rq, h)), codes(q)))
+                g.wait_ge(sem["rs%d" % h], n)
+                move((dst, OFF, s % "s", half(T.rp, h), p))
         g.wait_ge(sem.sent, sent[0])
         return
     if rank is None and core != add:
@@ -114,7 +134,7 @@ def rank_program(g, core, T, topo):
             if t not in known:
                 known[t] = 1
                 if t in lent:
-                    P.wait_ge(sem["wr%d" % t], 2 * ND)
+                    P.wait_ge(sem["wr%d" % t], lent[t])
                 else:
                     P.wait_ge(sem["w%d" % t], 1)
             wq, wp = wpart(t)
@@ -127,54 +147,60 @@ def rank_program(g, core, T, topo):
         return P.matmul_mx(bank(h, i), T.aq[:, 128 * i:128 * i + 128], T.ap[:, 128 * i:128 * i + 128],
                            T.bq[:, o:o + HC], T.bp[:, o:o + HC], k == 0, stop)
 
-    def cast_and_pack(h):
+    def cast_and_pack(h, vector=(0, 2), between=None):
         for i in range(4):
             out = T.st[:, 512 * h + i:512 * h + 512:4]
-            (V if i % 2 == 0 else S).wait_ge(sem["m%d%d" % (h, i)], 1)
-            if i % 2 == 0:
+            (V if i in vector else S).wait_ge(sem["m%d%d" % (h, i)], 1)
+            if i in vector:
                 V.tensor_copy(out, bank(h, i)).then_inc(sem["c%d%d" % (h, i)], 1)
             else:
                 S.activation(out, bank(h, i), COPY).then_inc(sem["c%d%d" % (h, i)], 1)
+        if between:
+            between()
         for i in range(4):
             V.wait_ge(sem["c%d%d" % (h, i)], 1)
         V.quantize_mx(half(T.sq, h), half(T.sp, h), T.st[:, 512 * h:512 * h + 512]).then_inc(sem["q%d" % h], 1)
 
-    def load_a(j):
-        g.sync.dma_start(T.at[:, 1024 * j:1024 * j + 1024], T.a[:, 1024 * j:1024 * j + 1024]).then_inc(sem["la%d" % j], 16)
+    def load_a(i, n):
+        g.sync.dma_start(T.at[:, 512 * i:512 * i + 512 * n], T.a[:, 512 * i:512 * i + 512 * n]).then_inc(sem["la%d" % i], 16)
 
     def load_b(k, h):
         o = 1024 * k + 512 * h
         g.sync.dma_start(T.bt[:, o:o + 512], T.b[:, o:o + 512]).then_inc(sem["lb%d%d" % (k, h)], 16)
 
     if rank is not None:
-        load_a(0)
+        load_a(0, 2)
         load_b(0, 0)
         load_b(1, 0)
-        load_a(1)
+        load_a(2, 1)
+        load_a(3, 1)
         load_b(0, 1)
         load_b(1, 1)
 
     if rank == 0:
-        constants([lend[core][1]])
+        constants(makes)
     else:
-        constants([t for t in (3, 0, 1, 2) if t not in lent])
+        constants(makes + [t for t in (3, 0, 1, 2) if t not in lent and t not in makes])
 
     if core == add:
-        P.wait_ge(sem.rc0, NR)
-        P.wait_ge(sem.rs0, NR)
+        g.wait_ge(sem.d0, 2 * ND)
+        move((C[2], ON, "d0", codes(half(T.dq, 0)), codes(half(T.dq, 0))))
+        move((C[2], ON, "d0", half(T.dp, 0), half(T.dp, 0)))
+        P.wait_ge(sem.rc0, ND + NR)
+        P.wait_ge(sem.rs0, ND + NR)
         unpack(half(T.rq, 0), half(T.rp, 0), 0, True, False)
         P.wait_ge(sem.d0, 2 * ND)
         unpack(half(T.dq, 0), half(T.dp, 0), 0, False, True, done="m")
         cast_and_pack(0)
         g.wait_ge(sem.q0, 1)
-        move((C[3], off_mask, "rc0", codes(half(T.sq, 0)), codes(half(T.rq, 0))))
-        move((C[3], off_mask, "rs0", half(T.sp, 0), half(T.rp, 0)))
+        move((C[3], OFF, "rc0", codes(half(T.sq, 0)), codes(half(T.rq, 0))))
+        move((C[3], OFF, "rs0", half(T.sp, 0), half(T.rp, 0)))
         g.wait_ge(sem.sent, sent[0])
         return
 
     def pack_a(i):
-        if i % 2 == 0:
-            V.wait_ge(sem["la%d" % (i // 2)], 16)
+        if i != 1:
+            V.wait_ge(sem["la%d" % i], 16)
         V.quantize_mx(T.aq[:, 128 * i:128 * i + 128], T.ap[:, 128 * i:128 * i + 128],
                       T.at[:, 512 * i:512 * i + 512]).then_inc(sem["a%d" % i], 1)
 
@@ -192,17 +218,17 @@ def rank_program(g, core, T, topo):
     def send(h):
         g.wait_ge(sem["q%d" % h], 1)
         q, p = half(T.sq, h), half(T.sp, h)
-        near = {0: r0, 1: r1, 2: add if h == 0 else r2}[rank]
-        c = [(near, on_mask, "rc%d" % h, codes(q), codes(half(T.rq, h)))]
-        s = [(near, on_mask, "rs%d" % h, p, half(T.rp, h))]
-        if rank == 0 and h == 0:
-            c.append((add, off_mask, "d0", codes(q), codes(half(T.dq, 0))))
-            s.append((add, off_mask, "d0", p, half(T.dp, 0)))
+        to = {0: [(r0b if h else r0, ON, "r"), (C[2] if h else add, OFF, "d")],
+              1: [(r1, ON, "r"), (C[3], OFF, "d")],
+              2: [(r2 if h else add, ALL, "r")]}[rank]
+
+        def put(to):
+            move(*[(d, m, "rc%d" % h if s == "r" else "d%d" % h, codes(q), codes(half(T[s + "q"], h))) for d, m, s in to])
+            move(*[(d, m, "rs%d" % h if s == "r" else "d%d" % h, p, half(T[s + "p"], h)) for d, m, s in to])
+
+        put(to)
         if rank == 0 and h == 1:
-            c.append((r0b, off_mask, "rc1", codes(q), codes(half(T.rq, 1))))
-            s.append((r0b, off_mask, "rs1", p, half(T.rp, 1)))
-        move(*c)
-        move(*s)
+            put([(r0, ON, "r")])
 
     pack_a(0)
     pack_a(1)
@@ -222,9 +248,10 @@ def rank_program(g, core, T, topo):
         own(0, 1, i)
     pack_b(0, 1)
     if rank != 3:
-        cast_and_pack(0)
+        cast_and_pack(0, (2,), lambda: pack_b(1, 1))
         send(0)
-    pack_b(1, 1)
+    else:
+        pack_b(1, 1)
     for k in range(2):
         P.wait_ge(sem["b%d1" % k], 1)
         for i in range(4):
@@ -232,12 +259,6 @@ def rank_program(g, core, T, topo):
     if rank != 3:
         cast_and_pack(1)
         send(1)
-    if rank == 0:
-        move((C[2], off_mask, "d0", codes(half(T.sq, 0)), codes(half(T.dq, 0))))
-        move((C[2], off_mask, "d0", half(T.sp, 0), half(T.dp, 0)))
-    elif rank == 1:
-        move((C[3], off_mask, "d", codes(T.sq[:, 0:256]), codes(T.dq[:, 0:256])))
-        move((C[3], off_mask, "d", T.sp[:, 0:256], T.dp[:, 0:256]))
 
     if rank in (1, 2):
         for h in range(2):
@@ -251,8 +272,9 @@ def rank_program(g, core, T, topo):
         P.wait_ge(sem["rs%d" % h], ND)
         unpack(half(T.rq, h), half(T.rp, h), h, False, stop, done="u" if stop else None)
 
-    def direct(h, stop):
-        unpack(half(T.dq, h), half(T.dp, h), h, False, stop, done="u" if stop else None)
+    def direct(h):
+        P.wait_ge(sem["d%d" % h], 2 * (NR if rank == 2 and h == 0 else ND))
+        unpack(half(T.dq, h), half(T.dp, h), h, False, False)
 
     def finish(h):
         for i in range(4):
@@ -265,6 +287,8 @@ def rank_program(g, core, T, topo):
                 S.activation(out, bank(h, i), COPY).then_inc(sem["e%d%d" % (h, i)], 1)
         for i in range(4):
             g.sync.wait_ge(sem["e%d%d" % (h, i)], 1)
+        if rank == 0 and h == 0:
+            g.sync.wait_ge(sem.sent, sent[0])
         g.sync.dma_start(T.y[:, 512 * h:512 * h + 512], T.yt[:, 512 * h:512 * h + 512]).then_inc(sem.stored, 16)
 
     if rank == 0:
@@ -276,14 +300,12 @@ def rank_program(g, core, T, topo):
             finish(h)
     elif rank == 2:
         for h in range(2):
-            relayed(h, False)
-            P.wait_ge(sem["d%d" % h], 2 * ND)
-            direct(h, True)
+            direct(h)
+            relayed(h, True)
             finish(h)
     else:
-        P.wait_ge(sem.d, 2 * ND)
-        direct(0, False)
-        direct(1, False)
+        direct(0)
+        direct(1)
         P.wait_ge(sem.xc, ND)
         P.wait_ge(sem.xs, ND)
         unpack(T.xq[:, 0:HC], T.xp[:, 0:HC], 1, False, False)

from concourse.bass import DstId, RemoteDMATransfer
from concourse.mybir import dt, AluOpType, ActivationFunctionType

HC = 128
LW = 32
X4 = "float8_e4m3fn_x4"
SCRATCH = {
    "at": ("sbuf", [128, 2048], "bfloat16"), "bt": ("sbuf", [128, 2048], "bfloat16"),
    "aq": ("sbuf", [128, 512], X4), "ap": ("sbuf", [128, 512], "uint8"),
    "bq": ("sbuf", [128, 512], X4), "bp": ("sbuf", [128, 512], "uint8"),
    "one": ("sbuf", [128, 128], "bfloat16"), "eye": ("sbuf", [128, 516], "bfloat16"),
    "wq": ("sbuf", [128, 512], X4), "wp": ("sbuf", [128, 512], "uint8"),
    "st": ("sbuf", [128, 1024], "bfloat16"),
    "sq": ("sbuf", [128, 256], X4), "sp": ("sbuf", [128, 256], "uint8"),
    "dq": ("sbuf", [128, 256], X4), "dp": ("sbuf", [128, 256], "uint8"),
    "rq": ("sbuf", [128, 256], X4), "rp": ("sbuf", [128, 256], "uint8"),
    "xq": ("sbuf", [128, 128], X4), "xp": ("sbuf", [128, 128], "uint8"),
    "yt": ("sbuf", [128, 1024], "float32"),
    "ps": ("psum", [128, 4096], "float32"),
}
SEMAPHORES = (["one", "eye", "la0", "la2", "la3", "sent", "stored", "xc", "xs", "wf0", "wf1"]
              + ["lb%d%d" % (k, h) for k in range(2) for h in range(2)]
              + ["w%d" % t for t in range(4)] + ["wr%d" % t for t in range(4)] + ["a%d" % i for i in range(4)]
              + ["b%d%d" % (k, h) for k in range(2) for h in range(2)]
              + ["%s%d%d" % (s, h, i) for s in ("m", "c", "u", "e") for h in range(2) for i in range(4)]
              + ["%s%d" % (s, h) for s in ("q", "d", "rc", "rs") for h in range(2)])


def _relay(src, dst, T, topo, same=True):
    for c in range(256):
        if (c not in T.cores and topo.host(c) == topo.host(src) and topo.chip(c) == topo.chip(src)
                and (topo.die(c) == topo.die(src)) == same and topo.may_write(c, dst)):
            return c


def rank_program(g, core, T, topo):
    C = list(T.cores)
    rank = T.rank_of(core)
    r0, r1, add = _relay(C[0], C[1], T, topo), _relay(C[1], C[2], T, topo), _relay(C[2], C[3], T, topo)
    r0b, r2 = _relay(C[0], C[3], T, topo, False), _relay(C[2], C[3], T, topo, False)
    sem = T.sem
    sent = [0]

    def bits(mask):
        return bin(mask).count("1")

    OFF = topo.mask(C[0], C[2])
    ALL = topo.mask(C[0], r0)
    ON = ALL & ~OFF
    ND, NR = bits(OFF), bits(ON)
    M, L = LW // 2, (LW + 128) // 2
    lend = [(C[0], r0, C[1], 1, 0, LW, ON), (r0b, None, C[1], 1, LW, 128, OFF), (r0, None, C[1], 0, 0, 128, OFF),
            (r1, None, C[1], 2, 0, 128, OFF),
            (C[1], r1, C[2], 3, 0, M, ON), (C[1], r1, C[2], 3, M, LW, OFF),
            (add, None, C[2], 3, LW, L, ON), (add, None, C[2], 3, L, 128, OFF),
            (C[0], None, add, 1, 0, LW, OFF), (r2, None, add, 1, LW, 128, OFF),
            (C[2], None, add, 2, 0, M, ON), (C[2], None, add, 2, M, LW, OFF), (r2, None, add, 2, LW, 128, OFF)]
    mine = [x for x in lend if x[0] == core]
    passed = [x for x in lend if x[1] == core]
    makes = sorted({x[3] for x in mine})
    lent = {}
    for t, piece, n in {(x[3], x[1] or x[4], bits(OFF if x[1] else x[6])) for x in lend if x[2] == core}:
        lent[t] = lent.get(t, 0) + 2 * n

    def half(t, h):
        return t[:, HC * h:HC * h + HC]

    def codes(ap):
        return ap.bitcast(dt.uint8)

    def move(*pairs):
        trs = []
        for d, mask, s, a, b in pairs:
            rid, pnc = topo.addr(d, core)
            trs.append(RemoteDMATransfer(dst_ids=[DstId(rid=rid, pnc=pnc)], dma_engine_mask=mask, remote_sem=sem[s],
                                         src=a, dst=b))
            sent[0] += bits(mask)
        g.remote_dma_fused(trs, local_sem=sem.sent)

    def wpart(t):
        return T.wq[:, 128 * t:128 * t + 128], T.wp[:, 128 * t:128 * t + 128]

    def piece(t, lo, hi, n):
        q, p = wpart(t)
        return p[:, lo:hi] if n else codes(q[:, lo:hi])

    def constants(ts):
        g.vector.memset(T.one[:], 1.0).then_inc(sem.one, 1)
        g.vector.memset(T.eye[:], 0.0).then_inc(sem.one, 1)
        g.wait_ge(sem.one, 2)
        g.affine_select(T.eye[:, 3:515:4], T.one[:], [[-1, 128]], AluOpType.is_equal, 0.0, 0, 1).then_inc(sem.eye, 1)
        g.vector.wait_ge(sem.eye, 1)
        for t in ts:
            q, p = wpart(t)
            g.vector.quantize_mx(q, p, T.eye[:, 3 - t:515 - t]).then_inc(sem["w%d" % t], 1)
        for t in makes:
            g.wait_ge(sem["w%d" % t], 1)
            for n in range(2):
                move(*[(v or d, mask, "wf%d" % n if v else "wr%d" % t, piece(t, lo, hi, n), piece(t, lo, hi, n))
                       for _, v, d, u, lo, hi, mask in mine if u == t])
        if passed:
            lo, hi, t, d = min(x[4] for x in passed), max(x[5] for x in passed), passed[0][3], passed[0][2]
            for n in range(2):
                g.wait_ge(sem["wf%d" % n], sum(bits(x[6]) for x in passed))
                move((d, OFF, "wr%d" % t, piece(t, lo, hi, n), piece(t, lo, hi, n)))

    relays = [(r0, 0, C[1]), (r0, 1, C[1]), (r0b, 1, C[3]), (r1, 0, C[2]), (r1, 1, C[2]), (r2, 1, C[3])]
    if core in (r0, r1, r0b, r2):
        constants(makes)
        n = ND + NR if core == r2 else NR
        for c, h, dst in relays:
            if c == core:
                q, p, s = (half(T.rq, h), half(T.rp, h), "r%s" + str(h)) if core != r2 else (half(T.xq, 0), half(T.xp, 0), "x%s")
                g.wait_ge(sem["rc%d" % h], n)
                move((dst, OFF, s % "c", codes(half(T.rq, h)), codes(q)))
                g.wait_ge(sem["rs%d" % h], n)
                move((dst, OFF, s % "s", half(T.rp, h), p))
        g.wait_ge(sem.sent, sent[0])
        return
    if rank is None and core != add:
        return

    V, S, P = g.vector, g.scalar, g.tensor
    COPY = ActivationFunctionType.Copy

    def bank(h, i):
        o = 512 * (4 * h + i)
        return T.ps[:, o:o + HC]

    known = {}

    def unpack(q, p, h, start, stop, done=None):
        for t in range(4):
            if t not in known:
                known[t] = 1
                if t in lent:
                    P.wait_ge(sem["wr%d" % t], lent[t])
                else:
                    P.wait_ge(sem["w%d" % t], 1)
            wq, wp = wpart(t)
            x = P.matmul_mx(bank(h, t), wq, wp, q, p, start, stop)
            if done:
                x.then_inc(sem["%s%d%d" % (done, h, t)], 1)

    def product(h, k, i, stop):
        o = 256 * k + HC * h
        return P.matmul_mx(bank(h, i), T.aq[:, 128 * i:128 * i + 128], T.ap[:, 128 * i:128 * i + 128],
                           T.bq[:, o:o + HC], T.bp[:, o:o + HC], k == 0, stop)

    def cast_and_pack(h, vector=(0, 2), between=None):
        for i in range(4):
            out = T.st[:, 512 * h + i:512 * h + 512:4]
            (V if i in vector else S).wait_ge(sem["m%d%d" % (h, i)], 1)
            if i in vector:
                V.tensor_copy(out, bank(h, i)).then_inc(sem["c%d%d" % (h, i)], 1)
            else:
                S.activation(out, bank(h, i), COPY).then_inc(sem["c%d%d" % (h, i)], 1)
        if between:
            between()
        for i in range(4):
            V.wait_ge(sem["c%d%d" % (h, i)], 1)
        V.quantize_mx(half(T.sq, h), half(T.sp, h), T.st[:, 512 * h:512 * h + 512]).then_inc(sem["q%d" % h], 1)

    def load_a(i, n):
        g.sync.dma_start(T.at[:, 512 * i:512 * i + 512 * n], T.a[:, 512 * i:512 * i + 512 * n]).then_inc(sem["la%d" % i], 16)

    def load_b(k, h):
        o = 1024 * k + 512 * h
        g.sync.dma_start(T.bt[:, o:o + 512], T.b[:, o:o + 512]).then_inc(sem["lb%d%d" % (k, h)], 16)

    if rank is not None:
        load_a(0, 2)
        load_b(0, 0)
        load_b(1, 0)
        load_a(2, 1)
        load_a(3, 1)
        load_b(0, 1)
        load_b(1, 1)

    if rank == 0:
        constants(makes)
    else:
        constants(makes + [t for t in (3, 0, 1, 2) if t not in lent and t not in makes])

    if core == add:
        g.wait_ge(sem.d0, 2 * ND)
        move((C[2], ON, "d0", codes(half(T.dq, 0)), codes(half(T.dq, 0))))
        move((C[2], ON, "d0", half(T.dp, 0), half(T.dp, 0)))
        P.wait_ge(sem.rc0, ND + NR)
        P.wait_ge(sem.rs0, ND + NR)
        unpack(half(T.rq, 0), half(T.rp, 0), 0, True, False)
        P.wait_ge(sem.d0, 2 * ND)
        unpack(half(T.dq, 0), half(T.dp, 0), 0, False, True, done="m")
        cast_and_pack(0)
        g.wait_ge(sem.q0, 1)
        move((C[3], OFF, "rc0", codes(half(T.sq, 0)), codes(half(T.rq, 0))))
        move((C[3], OFF, "rs0", half(T.sp, 0), half(T.rp, 0)))
        g.wait_ge(sem.sent, sent[0])
        return

    def pack_a(i):
        if i != 1:
            V.wait_ge(sem["la%d" % i], 16)
        V.quantize_mx(T.aq[:, 128 * i:128 * i + 128], T.ap[:, 128 * i:128 * i + 128],
                      T.at[:, 512 * i:512 * i + 512]).then_inc(sem["a%d" % i], 1)

    def pack_b(k, h):
        o = 256 * k + HC * h
        V.wait_ge(sem["lb%d%d" % (k, h)], 16)
        V.quantize_mx(T.bq[:, o:o + HC], T.bp[:, o:o + HC],
                      T.bt[:, 4 * o:4 * o + 512]).then_inc(sem["b%d%d" % (k, h)], 1)

    def own(h, k, i):
        x = product(h, k, i, k == 1 and rank != 3)
        if k == 1 and rank != 3:
            x.then_inc(sem["m%d%d" % (h, i)], 1)

    def send(h):
        g.wait_ge(sem["q%d" % h], 1)
        q, p = half(T.sq, h), half(T.sp, h)
        to = {0: [(r0b if h else r0, ON, "r"), (C[2] if h else add, OFF, "d")],
              1: [(r1, ON, "r"), (C[3], OFF, "d")],
              2: [(r2 if h else add, ALL, "r")]}[rank]

        def put(to):
            move(*[(d, m, "rc%d" % h if s == "r" else "d%d" % h, codes(q), codes(half(T[s + "q"], h))) for d, m, s in to])
            move(*[(d, m, "rs%d" % h if s == "r" else "d%d" % h, p, half(T[s + "p"], h)) for d, m, s in to])

        put(to)
        if rank == 0 and h == 1:
            put([(r0, ON, "r")])

    pack_a(0)
    pack_a(1)
    pack_b(0, 0)
    pack_b(1, 0)
    pack_a(2)
    pack_a(3)
    for k in range(2):
        P.wait_ge(sem["b%d0" % k], 1)
        for i in (0, 1):
            if k == 0:
                P.wait_ge(sem["a%d" % i], 1)
            own(0, k, i)
    for i in (2, 3):
        P.wait_ge(sem["a%d" % i], 1)
        own(0, 0, i)
        own(0, 1, i)
    pack_b(0, 1)
    if rank != 3:
        cast_and_pack(0, (2,), lambda: pack_b(1, 1))
        send(0)
    else:
        pack_b(1, 1)
    for k in range(2):
        P.wait_ge(sem["b%d1" % k], 1)
        for i in range(4):
            own(1, k, i)
    if rank != 3:
        cast_and_pack(1)
        send(1)

    if rank in (1, 2):
        for h in range(2):
            for i in range(4):
                P.wait_ge(sem["c%d%d" % (h, i)], 1)
                for k in range(2):
                    product(h, k, i, False)

    def relayed(h, stop):
        P.wait_ge(sem["rc%d" % h], ND)
        P.wait_ge(sem["rs%d" % h], ND)
        unpack(half(T.rq, h), half(T.rp, h), h, False, stop, done="u" if stop else None)

    def direct(h):
        P.wait_ge(sem["d%d" % h], 2 * (NR if rank == 2 and h == 0 else ND))
        unpack(half(T.dq, h), half(T.dp, h), h, False, False)

    def finish(h):
        for i in range(4):
            out = T.yt[:, 512 * h + i:512 * h + 512:4]
            e = V if i % 2 == 0 else S
            e.wait_ge(sem["%s%d%d" % ("u" if rank else "m", h, i)], 1)
            if i % 2 == 0:
                V.tensor_copy(out, bank(h, i)).then_inc(sem["e%d%d" % (h, i)], 1)
            else:
                S.activation(out, bank(h, i), COPY).then_inc(sem["e%d%d" % (h, i)], 1)
        for i in range(4):
            g.sync.wait_ge(sem["e%d%d" % (h, i)], 1)
        if rank == 0 and h == 0:
            g.sync.wait_ge(sem.sent, sent[0])
        g.sync.dma_start(T.y[:, 512 * h:512 * h + 512], T.yt[:, 512 * h:512 * h + 512]).then_inc(sem.stored, 16)

    if rank == 0:
        finish(0)
        finish(1)
    elif rank == 1:
        for h in range(2):
            relayed(h, True)
            finish(h)
    elif rank == 2:
        for h in range(2):
            direct(h)
            relayed(h, True)
            finish(h)
    else:
        direct(0)
        direct(1)
        P.wait_ge(sem.xc, ND)
        P.wait_ge(sem.xs, ND)
        unpack(T.xq[:, 0:HC], T.xp[:, 0:HC], 1, False, False)
        for h in (1, 0):
            relayed(h, True)
            finish(h)
    if sent[0]:
        g.wait_ge(sem.sent, sent[0])
    g.sync.wait_ge(sem.stored, 32)
